import numpy as np
import ml_dtypes


def mxq(x, axis, fmt="e4m3"):
    dtype, down = {"e4m3": (ml_dtypes.float8_e4m3fn, 7), "e5m2": (ml_dtypes.float8_e5m2, 14)}[fmt]
    v = np.moveaxis(np.asarray(x, np.float32).astype(ml_dtypes.bfloat16).astype(np.float64), axis, -1)
    blocks = v.reshape(v.shape[:-1] + (-1, 32))
    amax = np.abs(blocks).max(-1, keepdims=True)
    byte = np.maximum(np.where(amax > 0, np.frexp(amax)[1] - 1 + 127, 0) - down, 1)
    scale = np.exp2(byte - 127.0)
    codes = (blocks / scale).astype(np.float32).astype(dtype).astype(np.float64)
    return np.moveaxis((codes * scale).reshape(v.shape), -1, axis)


WIDE = False


def mx_kscale(k):
    if not WIDE:
        return np.ones(k)
    levels = np.array([10, -10, 5, -5, 0])
    if k % 512:
        return np.exp2(np.random.permutation(np.resize(levels, k // 32))).repeat(32)
    a = np.empty((k // 512, 16))
    for p in range(k // 512):
        a[p, :8] = np.random.permutation(np.resize(levels, 8))
        for g in range(8):
            far = levels[np.abs(levels - a[p, g]) >= 10]
            a[p, g + 8] = far[np.random.randint(len(far))]
    return np.exp2(a.ravel()).repeat(32)


def f64(x):
    return np.asarray(x).astype(np.float64)


def striped(idx):
    return np.tile(idx.reshape(-1, 16).T, (8, 1)).astype(np.uint16)


def unstriped(offs):
    return offs[:16].T.reshape(-1).astype(np.int64)


E2M1 = np.array([0.0, 0.5, 1.0, 1.5, 2.0, 3.0, 4.0, 6.0, -0.0, -0.5, -1.0, -1.5, -2.0, -3.0, -4.0, -6.0])


def pack_weight(w, fmt):
    k, n = w.shape
    w = f64(np.asarray(w, np.float32).astype(ml_dtypes.bfloat16)).reshape(k // 32, 32, n)
    amax = np.abs(w).max(1)
    if fmt == "e4m3":
        byte = np.frexp(amax)[1] - 1 + 127 - 7
    else:
        mant, ex = np.frexp(amax / 6.0)
        byte = np.where(mant > 0.5, ex, ex - 1) + 127
    byte = np.clip(np.where(amax > 0, byte, 1), 1, 254)
    scaled = (w * np.exp2(127.0 - byte)[:, None, :]).reshape(k, n).astype(np.float32)
    by_word = np.ascontiguousarray(scaled.reshape(k // 512, 128, 4, n).transpose(0, 1, 3, 2))
    if fmt == "e4m3":
        words = by_word.astype(ml_dtypes.float8_e4m3fn).view(np.uint8)
    else:
        c = by_word.astype(ml_dtypes.float4_e2m1fn).view(np.uint8) & 0xF
        words = (c[..., 0::2] | (c[..., 1::2] << 4)).reshape(k // 512, 128, 2 * n)
    return np.ascontiguousarray(words), np.ascontiguousarray(byte.astype(np.uint8).reshape(k // 512, 16, n))


def unpack_weight(words, scales, fmt):
    g, _, n = scales.shape
    words = np.ascontiguousarray(words).reshape(g, 128, n, -1)
    if fmt == "e4m3":
        vals = words.view(ml_dtypes.float8_e4m3fn).astype(np.float64)
    else:
        nib = np.empty((g, 128, n, 4), np.uint8)
        nib[..., 0::2] = words & 0xF
        nib[..., 1::2] = words >> 4
        vals = E2M1[nib]
    vals = vals * np.repeat(np.exp2(scales.astype(np.float64) - 127.0), 8, axis=1)[..., None]
    return vals.transpose(0, 1, 3, 2).reshape(g * 512, n)


def gelu(v):
    return 0.5 * v * (1.0 + np.tanh(np.sqrt(2.0 / np.pi) * (v + 0.044715 * v**3)))


K, K2, T, T2, S, P, H, N = 1024, 512, 4096, 2048, 1024, 512, 1024, 512

def setup_inputs():
    n = np.random.standard_normal
    s = mx_kscale(K)[:, None]
    s2 = mx_kscale(K2)[:, None]
    u = mx_kscale(H)[:, None]
    d = {}
    d["tab_words"], d["tab_scales"] = pack_weight(n((K, T)) * s, "e4m3")
    d["offs"] = striped(np.random.permutation(T)[:S])
    d["tab2_words"], d["tab2_scales"] = pack_weight(n((K2, T2)) * s2, "e4m3")
    d["offs2"] = striped(np.random.permutation(T2)[:P])
    d["pos1"] = striped(np.random.permutation(S)[:P])
    d["w1"] = (n((K, H)) / K ** 0.5 / s * u.T).astype(np.float32)
    d["w4_words"], d["w4_scales"] = pack_weight(0.29 * n((K2, H)) / K2 ** 0.5 / s2, "e2m1")
    d["phase"] = np.random.uniform(-0.85, 0.85, H).astype(np.float32)
    d["wgs"] = np.exp(0.3 * np.clip(n((128, P)), -1.0, 1.0)).astype(np.float32)
    d["shape0"] = (0.6 * n((H, S)) * u).astype(np.float32)
    d["w2"] = (2.0 * n((H, N)) / H ** 0.5 / u).astype(np.float32)
    return d

def reference(tab_words, tab_scales, offs, tab2_words, tab2_scales, offs2, pos1, w1, w4_words, w4_scales, phase, wgs, shape0, w2):
    v = unpack_weight(tab_words, tab_scales, "e4m3")[:, unstriped(offs)]
    v2 = unpack_weight(tab2_words, tab2_scales, "e4m3")[:, unstriped(offs2)]
    w4 = unpack_weight(w4_words, w4_scales, "e2m1")
    a = mxq(f64(w1), 0, "e4m3").T @ v
    b = (w4.T @ v2) + f64(phase)[:, None]
    placed = np.zeros((H, S))
    placed[:, unstriped(pos1)] = np.tile(f64(wgs), (H // 128, 1)) * b
    z = a * np.cos(placed) + f64(shape0)
    y = mxq(f64(w2), 0, "e4m3").T @ mxq(z, 0, "e4m3")
    return np.sqrt(1.0 + np.square(y))

@@ -1,0 +1,344 @@
+import math
+from contextlib import ExitStack
+
+import concourse.mybir as mybir
+from concourse.masks import make_identity
+
+K, K2, T, T2, S, NP, H, N = 1024, 512, 4096, 2048, 1024, 512, 1024, 512
+FLOPS = 2 * (K * H * S + K2 * H * NP + H * N * S)
+
+F32 = mybir.dt.float32
+BF16 = mybir.dt.bfloat16
+I32 = mybir.dt.int32
+U32 = mybir.dt.uint32
+U16 = mybir.dt.uint16
+U8 = mybir.dt.uint8
+FP8X4 = mybir.dt.float8_e4m3fn_x4
+FP4X4 = mybir.dt.float4_e2m1fn_x4
+ACT = mybir.ActivationFunctionType
+MULT = mybir.AluOpType.mult
+ADD = mybir.AluOpType.add
+
+P = 128
+BANK = 512
+CHUNK = 256
+W1_SLOT = [["late0", "cos0"], ["cos1", "late1"]]
+CHUNKS = [(0, 256), (256, 256), (512, 256), (768, 128), (896, 128)]
+
+
+def tile_list_lens_surface_correction_kernel(
+    tc, tab_words, tab_scales, offs, tab2_words, tab2_scales, offs2, pos1, w1, w4_words, w4_scales,
+    phase, wgs, shape0, w2, out,
+):
+    nc = tc.nc
+    with ExitStack() as ctx:
+        keep = ctx.enter_context(tc.tile_pool(name="keep", bufs=1))
+        ring = ctx.enter_context(tc.tile_pool(name="ring", bufs=2))
+        psum = ctx.enter_context(tc.psum_pool(name="psum", bufs=1))
+
+        def kept(name, shape, dtype):
+            return keep.tile(shape, dtype, name=name, align_bytes=64)
+
+        banks = [psum.tile([P, BANK], F32, name="bank%d" % i) for i in range(8)]
+
+        idx = keep.tile([P, S // 16], U16, name="idx")
+        idx2 = keep.tile([P, NP // 16], U16, name="idx2")
+        places = keep.tile([P, NP // 16], U16, name="places")
+        tab_w = [kept("tab_w%d" % a, [P, T], I32) for a in range(2)]
+        tab_s = kept("tab_s", [P, T], U8)
+        tab2_w = kept("tab2_w", [P, T2], I32)
+        tab2_s = kept("tab2_s", [P, T2], U8)
+        v_w = [kept("v_w%d" % a, [P, S], U32) for a in range(2)]
+        v_s = kept("v_s", [P, S], U8)
+        v2_w = kept("v2_w", [P, NP], U32)
+        v2_s = kept("v2_s", [P, NP], U8)
+        w4_w = kept("w4_w", [P, 2 * H], U8)
+        w4_s = kept("w4_s", [P, H], U8)
+        w4_dealt_w = kept("w4_dealt_w", [P, H], U8)
+        w4_dealt_s = kept("w4_dealt_s", [P, H // 2], U8)
+        phase_rows = kept("phase_rows", [P, 4], F32)
+        wgs_rows = kept("wgs_rows", [P, NP], F32)
+        wgs_dealt = kept("wgs_dealt", [P, 4, NP], F32)
+        s0_rows = [kept("s0_rows%d" % s, [P, S], F32) for s in range(4)]
+        s0_dealt = kept("s0_dealt", [P, 4, S], F32)
+        w1_w = [[kept("w1_w%d%d" % (b, a), [P, 512], U32) for a in range(2 - b)] for b in range(2)]
+        w1_s = [[kept("w1_s%d%d" % (b, a), [P, 512], U8) for a in range(2)] for b in range(2)]
+        w2_w = []
+        w2_s = [kept("w2_s%d" % b, [P, N], U8) for b in range(2)]
+        z_w = [kept("z_w%d" % b, [P, S], U32) for b in range(2)]
+        z_s = [kept("z_s%d" % b, [P, S], U8) for b in range(2)]
+        pages = [kept("page%d" % i, [P, S + 16], F32) for i in range(4)]
+        z_turned = [kept("z_turned%d" % h, [P, 4, 2, P, 2], BF16) for h in range(2)]
+        ident = kept("ident", [P, P], F32)
+        zero = kept("zero", [P, 1], F32)
+        sin_zero = kept("sin_zero", [P, 1], F32)
+        half_pi = kept("half_pi", [P, 1], F32)
+        one = kept("one", [P, 1], F32)
+        root_one = kept("root_one", [P, 1], F32)
+
+        def load_scale_rows(queue, plane, scales):
+            passes = scales.shape[0]
+            for q in range(4):
+                queue.dma_start(
+                    out=plane[32 * q : 32 * q + 4 * passes, :].bitcast(I32),
+                    in_=scales[:, 4 * q : 4 * q + 4, :].bitcast(I32),
+                )
+
+        def load_weight(rows, tag):
+            raw = keep.tile([P, 4 * 512], F32, name="raw", tag=tag)
+            nc.sync.dma_start(
+                out=raw[:, 0:2048].rearrange("p (j c) -> p j c", j=4), in_=rows.rearrange("(p j) c -> p j c", j=4)
+            )
+            return raw
+
+        def load_scale_rows_repeated(plane, scales):
+            for q in range(4):
+                nc.sync.dma_start(
+                    out=plane[32 * q : 32 * (q + 1), :].bitcast(I32),
+                    in_=scales[0, 4 * q : 4 * q + 4, :].bitcast(I32).partition_broadcast(8),
+                )
+
+        nc.vector.memset(zero[:], 0.0)
+        nc.vector.memset(one[:], 1.0)
+        nc.scalar.activation(out=sin_zero[:], in_=zero[:], func=ACT.Sin)
+        nc.gpsimd.memset(tab_s[:].bitcast(I32), 0)
+        for i, page in enumerate(pages):
+            (nc.vector if i < 2 else nc.gpsimd).memset(page[:], 0.0)
+        nc.vector.tensor_scalar_add(half_pi[:], sin_zero[:], math.pi / 2)
+        make_identity(nc, ident[:])
+
+        nc.sync.dma_start(idx2[:], offs2)
+        load_scale_rows_repeated(tab2_s, tab2_scales)
+        with nc.allow_non_contiguous_dma(reason="one phase value a partition"):
+            nc.sync.dma_start(out=phase_rows[:], in_=phase[0:512].rearrange("(s p) -> p s", p=P))
+        nc.sync.dma_start(out=w4_w[:].bitcast(I32), in_=w4_words[0].bitcast(I32))
+        nc.sync.dma_start(out=tab2_w[:], in_=tab2_words[0].rearrange("p t i -> p (t i)").bitcast(I32))
+        load_scale_rows_repeated(w4_s, w4_scales)
+        nc.sync.dma_start(places[:], pos1)
+        nc.sync.dma_start(out=wgs_rows[:], in_=wgs)
+        nc.sync.dma_start(idx[:], offs)
+
+        def load_table(a):
+            nc.sync.dma_start(out=tab_w[a][:], in_=tab_words[a].rearrange("p t i -> p (t i)").bitcast(I32))
+
+        def load_shape_rows(s):
+            nc.sync.dma_start(out=s0_rows[s][:], in_=shape0[P * s : P * (s + 1), :])
+
+        w1_raw = [[None, None], [None, None]]
+        for b in range(2):
+            for a in range(2):
+                w1_raw[b][a] = load_weight(w1[512 * a : 512 * (a + 1), 512 * b : 512 * (b + 1)], W1_SLOT[b][a])
+            if b == 1:
+                load_scale_rows(nc.sync, tab_s, tab_scales)
+            load_table(b)
+        cosines1 = keep.tile([P, 2 * S + 8], F32, name="cosines1", tag="cos1")
+        phase_dealt = cosines1[:, 2 * S : 2 * S + 4]
+        with nc.allow_non_contiguous_dma(reason="four phase values a partition"):
+            nc.sync.dma_start(out=phase_dealt, in_=phase[512:1024].rearrange("(p t) -> p t", t=4))
+        w2_raw = []
+        for b in range(2):
+            w2_raw.append(load_weight(w2[512 * b : 512 * (b + 1), :], ("late0", "w2_second")[b]))
+            load_shape_rows(b)
+        for q in range(4):
+            nc.sync.dma_start(
+                out=wgs_dealt[32 * q : 32 * (q + 1), :, :], in_=wgs.rearrange("(p t) j -> p t j", t=4)
+            )
+        for s in range(2, 4):
+            load_shape_rows(s)
+        nc.sync.dma_start(out=s0_dealt[:], in_=shape0[512:1024, :].rearrange("(p t) j -> p t j", t=4))
+
+        def gather(dst, window, offsets):
+            nc.vector.tensor_copy(dst, window.indirect(offsets))
+
+        def quantise(codes, scales, grouped):
+            nc.vector.quantize_mx(out=codes.bitcast(FP8X4), scales=scales, in_=grouped)
+
+        def round_weight(raw, deal):
+            grouped = ring.tile([P, 512, 4], BF16, name="grouped", bufs=3, align_bytes=64)
+            if deal:
+                dst = grouped[:].rearrange("p (t m) j -> p m j t", t=4)
+                src = raw[:, 0:2048].rearrange("p (j m t) -> p m j t", j=4, t=4)
+            else:
+                dst = grouped[:].rearrange("p (c i) j -> p c j i", i=4)
+                src = raw[:, 0:2048].rearrange("p (j c i) -> p c j i", j=4, i=4)
+            for half in range(2):
+                nc.scalar.copy(out=dst[:, 64 * half : 64 * (half + 1)], in_=src[:, 64 * half : 64 * (half + 1)])
+            return grouped[:].rearrange("p c j -> p (c j)")
+
+        def phase_features(s, bank):
+            b, t = divmod(s, 4)
+            words, scales = (w4_w, w4_s) if b == 0 else (w4_dealt_w, w4_dealt_s)
+            bias = (phase_rows, phase_dealt)[b][:, t : t + 1]
+            nc.tensor.matmul_mx(
+                out=bank[:], lhsT=words[:, 2 * P * t : 2 * P * (t + 1)].bitcast(FP4X4),
+                lhsT_scale=scales[:, P * t : P * (t + 1)], rhs=v2_w[:].bitcast(FP8X4), rhs_scale=v2_s[:],
+                start=True, stop=True,
+            )
+            b_abs = keep.tile([P, NP], F32, name="b_abs", tag="b_abs%d" % t, align_bytes=64)
+            nc.scalar.activation(out=b_abs[:], in_=bank[:], func=ACT.Abs, bias=bias)
+            return b_abs
+
+        def cosine(s):
+            return cosines[s % 4 // 2][:, S * (s % 2) : S * (s % 2 + 1)]
+
+        def place_phases(s, b_abs):
+            b, t = divmod(s, 4)
+            weights = wgs_rows[:] if b == 0 else wgs_dealt[:, t, :]
+            page = pages[t]
+            nc.vector.tensor_tensor(page[:].indirect(places[:]), b_abs[:], weights, MULT)
+
+        def take_cosine(s):
+            nc.scalar.activation(out=cosine(s), in_=pages[s % 4][:, 0:S], func=ACT.Sin, scale=-1.0, bias=half_pi[:])
+
+        def features(acc, b, t, cols):
+            for a in range(2):
+                nc.tensor.matmul_mx(
+                    out=acc, lhsT=w1_w[b][a][:, P * t : P * (t + 1)].bitcast(FP8X4),
+                    lhsT_scale=w1_s[b][a][:, P * t : P * (t + 1)],
+                    rhs=v_w[a][:, cols].bitcast(FP8X4), rhs_scale=v_s[4 * a : P, cols],
+                    start=(a == 0), stop=(a == 1),
+                )
+
+        def first_half_product(s, h):
+            cols = slice(BANK * h, BANK * (h + 1))
+            acc = banks[(2 * s + h) % 4]
+            features(acc[:], 0, s, cols)
+            prod = ring.tile([P, BANK], F32, name="prod", bufs=4)
+            page = pages[h + 2 * (s // 3)]
+            nc.vector.scalar_tensor_tensor(prod[:], acc[:], page[:, S : S + 1], cosine(s)[:, cols], ADD, MULT)
+            return prod
+
+        def first_half_turn(s, h, prod):
+            turned = banks[4 + (2 * s + h) % 4]
+            for jb in range(4):
+                blk = slice(P * jb, P * (jb + 1))
+                nc.tensor.matmul(
+                    turned[:, blk], lhsT=s0_rows[s][:, BANK * h + P * jb : BANK * h + P * (jb + 1)],
+                    rhs=ident[:], is_transpose=True, start=True, stop=False,
+                )
+                nc.tensor.matmul(
+                    turned[:, blk], lhsT=prod[:, blk], rhs=ident[:], is_transpose=True, start=False, stop=True
+                )
+            nc.scalar.copy(
+                out=z_turned[h][:, :, :, 32 * s : 32 * (s + 1), :],
+                in_=turned[:].rearrange("p (b q u e) -> p b u q e", b=4, u=2, e=2),
+            )
+
+        def first_half_back(c):
+            h, pair = divmod(c, 2)
+            words = z_turned[h][:].rearrange("p b u q e -> p (b u q e)").bitcast(F32)
+            bank = banks[6 + c % 2]
+            for i in range(4):
+                at = P * (4 * pair + i)
+                nc.tensor.transpose(bank[:, P * i : P * (i + 1)], words[:, at : at + P], ident[:])
+            grouped = ring.tile([P, 4 * CHUNK], BF16, name="z_grouped0", align_bytes=64)
+            nc.scalar.copy(
+                out=grouped[:].bitcast(F32).rearrange("p (b j u) -> p b j u", b=2, u=2),
+                in_=bank[:].rearrange("p (b u j) -> p b j u", b=2, u=2),
+            )
+            cols = slice(CHUNK * c, CHUNK * (c + 1))
+            quantise(z_w[0][:, cols], z_s[0][:, cols], grouped[:])
+
+        def second_half_products(c, k, prod):
+            start, width = CHUNKS[c]
+            cols = slice(start, start + width)
+            acc = banks[2 * (c % 2) + k]
+            for i in range(2):
+                features(acc[:, width * i : width * (i + 1)], 1, 2 * k + i, cols)
+            nc.vector.tensor_tensor(
+                prod[:, 2 * k : 2 * k + 2, 0:width], acc[:, 0 : 2 * width].rearrange("p (t j) -> p t j", t=2),
+                cosines[k][:, 0 : 2 * S].rearrange("p (t j) -> p t j", t=2)[:, :, cols], MULT,
+            )
+
+        def second_half_sum(c, prod):
+            start, width = CHUNKS[c]
+            grouped = ring.tile([P, CHUNK, 4], BF16, name="z_grouped1", align_bytes=64)
+            nc.vector.tensor_tensor(
+                grouped[:, 0:width, :].rearrange("p (c i) t -> p c t i", i=2),
+                prod[:, :, 0:width].rearrange("p t (c i) -> p c t i", i=2),
+                s0_dealt[:, :, start : start + width].rearrange("p t (c i) -> p c t i", i=2),
+                ADD,
+            )
+            return grouped
+
+        def finish_chunk(c, grouped):
+            start, width = CHUNKS[c]
+            cols = slice(start, start + width)
+            quantise(z_w[1][:, cols], z_s[1][:, cols], grouped[:, 0:width, :].rearrange("p j t -> p (j t)"))
+            for k in range(2):
+                acc = banks[4 + 2 * (c % 2) + k]
+                for i in range(2):
+                    n_cols = slice(P * (2 * k + i), P * (2 * k + i + 1))
+                    for b in range(2):
+                        nc.tensor.matmul_mx(
+                            out=acc[:, width * i : width * (i + 1)], lhsT=w2_w[b][:, n_cols].bitcast(FP8X4),
+                            lhsT_scale=w2_s[b][:, n_cols], rhs=z_w[b][:, cols].bitcast(FP8X4),
+                            rhs_scale=z_s[b][:, cols], start=(b == 0), stop=(b == 1),
+                        )
+                squares = ring.tile([P, BANK], F32, name="squares")
+                nc.scalar.activation(out=squares[:, 0 : 2 * width], in_=acc[:, 0 : 2 * width], func=ACT.Square)
+                result = ring.tile([P, BANK], F32, name="result", bufs=3)
+                nc.scalar.activation(
+                    out=result[:, 0 : 2 * width], in_=squares[:, 0 : 2 * width], func=ACT.Sqrt, bias=root_one[:]
+                )
+                nc.sync.dma_start(
+                    out=out[2 * P * k : 2 * P * (k + 1), cols].rearrange("(m p) j -> p m j", p=P),
+                    in_=result[:, 0 : 2 * width].rearrange("p (m j) -> p m j", m=2),
+                )
+
+        gather(v2_w[:], tab2_w[:].bitcast(U32), idx2[:])
+        gather(v2_s[:], tab2_s[:], idx2[:])
+        nc.vector.tensor_copy(
+            w4_dealt_w[:].bitcast(U16).rearrange("p (t m) -> p t m", t=4),
+            w4_w[:, H : 2 * H].bitcast(U16).rearrange("p (m t) -> p t m", t=4),
+        )
+        nc.vector.tensor_copy(
+            w4_dealt_s[:].rearrange("p (t m) -> p t m", t=4),
+            w4_s[:, H // 2 : H].rearrange("p (m t) -> p t m", t=4),
+        )
+        b_abs = [phase_features(s, banks[6 + s % 2]) for s in range(2)]
+        rounded = [round_weight(w1_raw[0][a], False) for a in range(2)]
+        cosines = [keep.tile([P, 2 * S], F32, name="cosines0", tag="cos0"), cosines1]
+        for s in range(2):
+            place_phases(s, b_abs[s])
+            take_cosine(s)
+        for a in range(2):
+            quantise(w1_w[0][a][:], w1_s[0][a][:], rounded[a])
+        b_abs = [phase_features(s, banks[6 + s % 2]) for s in range(2, 4)]
+        rounded = [round_weight(w1_raw[1][a], True) for a in range(2)]
+        for s in range(2, 4):
+            place_phases(s, b_abs[s - 2])
+            take_cosine(s)
+        gather(v_w[0][:], tab_w[0][:].bitcast(U32), idx[:])
+        quantise(w1_w[1][0][:], w1_s[1][0][:], rounded[0])
+        b_abs = [phase_features(s, banks[6 + s % 2]) for s in range(4, 8)]
+        gather(v_s[:], tab_s[:], idx[:])
+        for h in range(2):
+            gather(v_w[1][:, BANK * h : BANK * (h + 1)], tab_w[1][:].bitcast(U32), idx[:, 32 * h : 32 * (h + 1)])
+        waiting = [(w1_w[1], w1_s[1][1], rounded[1])]
+        waiting.extend((w2_w, w2_s[b], round_weight(w2_raw[b], False)) for b in range(2))
+        for g in range(2):
+            halves = [(s, h) for s in (2 * g, 2 * g + 1) for h in range(2)]
+            prods = [first_half_product(s, h) for s, h in halves]
+            for (s, h), prod in zip(halves, prods):
+                first_half_turn(s, h, prod)
+            for t in (2 * g, 2 * g + 1):
+                place_phases(4 + t, b_abs[t])
+                take_cosine(4 + t)
+                if t < 3:
+                    holder, scales, values = waiting[t]
+                    codes = keep.tile([P, 512], U32, name="codes", tag="b_abs%d" % t, align_bytes=64)
+                    holder.append(codes)
+                    quantise(codes[:], scales[:], values)
+        nc.scalar.activation(out=root_one[:], in_=cosine(7)[:, 0:1], func=ACT.Sqrt, scale=0.0, bias=one[:])
+        for c in range(4):
+            first_half_back(c)
+        grouped = None
+        for c in range(len(CHUNKS)):
+            prod = keep.tile([P, 4, CHUNK], F32, name="prod4", tag="late%d" % (c % 2))
+            second_half_products(c, 0, prod)
+            if c > 0:
+                finish_chunk(c - 1, grouped)
+            second_half_products(c, 1, prod)
+            grouped = second_half_sum(c, prod)
+        finish_chunk(len(CHUNKS) - 1, grouped)

@@ -59,7 +59,7 @@ def tile_list_lens_surface_correction_kernel(
         phase_rows = kept("phase_rows", [P, 4], F32)
         wgs_rows = kept("wgs_rows", [P, NP], F32)
         wgs_dealt = kept("wgs_dealt", [P, 4, NP], F32)
-        s0_rows = [kept("s0_rows%d" % s, [P, S], F32) for s in range(4)]
+        s0_rows = [keep.tile([P, S], F32, name="s0_rows", tag="rows%d" % s) for s in range(4)]
         s0_dealt = kept("s0_dealt", [P, 4, S], F32)
         w1_w = [[kept("w1_w%d%d" % (b, a), [P, 512], U32) for a in range(2 - b)] for b in range(2)]
         w1_s = [[kept("w1_s%d%d" % (b, a), [P, 512], U8) for a in range(2)] for b in range(2)]
@@ -108,11 +108,11 @@ def tile_list_lens_surface_correction_kernel(
         make_identity(nc, ident[:])
 
         nc.sync.dma_start(idx2[:], offs2)
-        load_scale_rows_repeated(tab2_s, tab2_scales)
-        with nc.allow_non_contiguous_dma(reason="one phase value a partition"):
-            nc.sync.dma_start(out=phase_rows[:], in_=phase[0:512].rearrange("(s p) -> p s", p=P))
-        nc.sync.dma_start(out=w4_w[:].bitcast(I32), in_=w4_words[0].bitcast(I32))
         nc.sync.dma_start(out=tab2_w[:], in_=tab2_words[0].rearrange("p t i -> p (t i)").bitcast(I32))
+        with nc.allow_non_contiguous_dma(reason="one phase value a partition"):
+            nc.scalar.dma_start(out=phase_rows[:], in_=phase[0:512].rearrange("(s p) -> p s", p=P))
+        load_scale_rows_repeated(tab2_s, tab2_scales)
+        nc.sync.dma_start(out=w4_w[:].bitcast(I32), in_=w4_words[0].bitcast(I32))
         load_scale_rows_repeated(w4_s, w4_scales)
         nc.sync.dma_start(places[:], pos1)
         nc.sync.dma_start(out=wgs_rows[:], in_=wgs)
@@ -156,8 +156,11 @@ def tile_list_lens_surface_correction_kernel(
         def round_weight(raw, deal):
             grouped = ring.tile([P, 512, 4], BF16, name="grouped", bufs=3, align_bytes=64)
             if deal:
-                dst = grouped[:].rearrange("p (t m) j -> p m j t", t=4)
-                src = raw[:, 0:2048].rearrange("p (j m t) -> p m j t", j=4, t=4)
+                dst = grouped[:].rearrange("p (u e m) j -> p u m j e", u=2, e=2)
+                src = raw[:, 0:2048].rearrange("p (j m u e) -> p u m j e", j=4, u=2, e=2)
+                for u in range(2):
+                    nc.scalar.copy(out=dst[:, u], in_=src[:, u])
+                return grouped[:].rearrange("p c j -> p (c j)")
             else:
                 dst = grouped[:].rearrange("p (c i) j -> p c j i", i=4)
                 src = raw[:, 0:2048].rearrange("p (j c i) -> p c j i", j=4, i=4)
@@ -199,10 +202,12 @@ def tile_list_lens_surface_correction_kernel(
                     start=(a == 0), stop=(a == 1),
                 )
 
+        def first_half_features(s, h):
+            features(banks[(2 * s + h) % 4][:], 0, s, slice(BANK * h, BANK * (h + 1)))
+
         def first_half_product(s, h):
             cols = slice(BANK * h, BANK * (h + 1))
             acc = banks[(2 * s + h) % 4]
-            features(acc[:], 0, s, cols)
             prod = ring.tile([P, BANK], F32, name="prod", bufs=4)
             page = pages[h + 2 * (s // 3)]
             nc.vector.scalar_tensor_tensor(prod[:], acc[:], page[:, S : S + 1], cosine(s)[:, cols], ADD, MULT)
@@ -231,7 +236,7 @@ def tile_list_lens_surface_correction_kernel(
             for i in range(4):
                 at = P * (4 * pair + i)
                 nc.tensor.transpose(bank[:, P * i : P * (i + 1)], words[:, at : at + P], ident[:])
-            grouped = ring.tile([P, 4 * CHUNK], BF16, name="z_grouped0", align_bytes=64)
+            grouped = ring.tile([P, 4 * CHUNK], BF16, name="z_grouped0", bufs=4, align_bytes=64)
             nc.scalar.copy(
                 out=grouped[:].bitcast(F32).rearrange("p (b j u) -> p b j u", b=2, u=2),
                 in_=bank[:].rearrange("p (b u j) -> p b j u", b=2, u=2),
@@ -254,9 +259,9 @@ def tile_list_lens_surface_correction_kernel(
             start, width = CHUNKS[c]
             grouped = ring.tile([P, CHUNK, 4], BF16, name="z_grouped1", align_bytes=64)
             nc.vector.tensor_tensor(
-                grouped[:, 0:width, :].rearrange("p (c i) t -> p c t i", i=2),
-                prod[:, :, 0:width].rearrange("p t (c i) -> p c t i", i=2),
-                s0_dealt[:, :, start : start + width].rearrange("p t (c i) -> p c t i", i=2),
+                grouped[:, 0:width, :].rearrange("p (c i) t -> p c t i", i=4),
+                prod[:, :, 0:width].rearrange("p t (c i) -> p c t i", i=4),
+                s0_dealt[:, :, start : start + width].rearrange("p t (c i) -> p c t i", i=4),
                 ADD,
             )
             return grouped
@@ -265,7 +270,9 @@ def tile_list_lens_surface_correction_kernel(
             start, width = CHUNKS[c]
             cols = slice(start, start + width)
             quantise(z_w[1][:, cols], z_s[1][:, cols], grouped[:, 0:width, :].rearrange("p j t -> p (j t)"))
+            results = keep.tile([P, 2, BANK], F32, name="results", tag=("rows%d" % c if c < 4 else "w2_second"))
             for k in range(2):
+                result = results[:, k, :]
                 acc = banks[4 + 2 * (c % 2) + k]
                 for i in range(2):
                     n_cols = slice(P * (2 * k + i), P * (2 * k + i + 1))
@@ -277,7 +284,6 @@ def tile_list_lens_surface_correction_kernel(
                         )
                 squares = ring.tile([P, BANK], F32, name="squares")
                 nc.scalar.activation(out=squares[:, 0 : 2 * width], in_=acc[:, 0 : 2 * width], func=ACT.Square)
-                result = ring.tile([P, BANK], F32, name="result", bufs=3)
                 nc.scalar.activation(
                     out=result[:, 0 : 2 * width], in_=squares[:, 0 : 2 * width], func=ACT.Sqrt, bias=root_one[:]
                 )
@@ -317,9 +323,15 @@ def tile_list_lens_surface_correction_kernel(
             gather(v_w[1][:, BANK * h : BANK * (h + 1)], tab_w[1][:].bitcast(U32), idx[:, 32 * h : 32 * (h + 1)])
         waiting = [(w1_w[1], w1_s[1][1], rounded[1])]
         waiting.extend((w2_w, w2_s[b], round_weight(w2_raw[b], False)) for b in range(2))
+        for s in range(2):
+            for h in range(2):
+                first_half_features(s, h)
         for g in range(2):
             halves = [(s, h) for s in (2 * g, 2 * g + 1) for h in range(2)]
             prods = [first_half_product(s, h) for s, h in halves]
+            if g == 0:
+                for s, h in halves:
+                    first_half_features(s + 2, h)
             for (s, h), prod in zip(halves, prods):
                 first_half_turn(s, h, prod)
             for t in (2 * g, 2 * g + 1):
@@ -330,9 +342,9 @@ def tile_list_lens_surface_correction_kernel(
                     codes = keep.tile([P, 512], U32, name="codes", tag="b_abs%d" % t, align_bytes=64)
                     holder.append(codes)
                     quantise(codes[:], scales[:], values)
-        nc.scalar.activation(out=root_one[:], in_=cosine(7)[:, 0:1], func=ACT.Sqrt, scale=0.0, bias=one[:])
         for c in range(4):
             first_half_back(c)
+        nc.scalar.activation(out=root_one[:], in_=cosine(7)[:, 0:1], func=ACT.Sqrt, scale=0.0, bias=one[:])
         grouped = None
         for c in range(len(CHUNKS)):
             prod = keep.tile([P, 4, CHUNK], F32, name="prod4", tag="late%d" % (c % 2))

@@ -57,11 +57,11 @@ def tile_list_lens_surface_correction_kernel(
         w4_dealt_w = kept("w4_dealt_w", [P, H], U8)
         w4_dealt_s = kept("w4_dealt_s", [P, H // 2], U8)
         phase_rows = kept("phase_rows", [P, 4], F32)
-        wgs_rows = kept("wgs_rows", [P, NP], F32)
+        wgs_rows = keep.tile([P, NP], F32, name="wgs_rows", tag="wgs_rows", align_bytes=64)
         wgs_dealt = kept("wgs_dealt", [P, 4, NP], F32)
         s0_rows = [keep.tile([P, S], F32, name="s0_rows", tag="rows%d" % s) for s in range(4)]
         s0_dealt = kept("s0_dealt", [P, 4, S], F32)
-        w1_w = [[kept("w1_w%d%d" % (b, a), [P, 512], U32) for a in range(2 - b)] for b in range(2)]
+        w1_w = [[], [kept("w1_w10", [P, 512], U32)]]
         w1_s = [[kept("w1_s%d%d" % (b, a), [P, 512], U8) for a in range(2)] for b in range(2)]
         w2_w = []
         w2_s = [kept("w2_s%d" % b, [P, N], U8) for b in range(2)]
@@ -73,6 +73,7 @@ def tile_list_lens_surface_correction_kernel(
         zero = kept("zero", [P, 1], F32)
         sin_zero = kept("sin_zero", [P, 1], F32)
         half_pi = kept("half_pi", [P, 1], F32)
+        half_pi_late = kept("half_pi_late", [P, 1], F32)
         one = kept("one", [P, 1], F32)
         root_one = kept("root_one", [P, 1], F32)
 
@@ -91,8 +92,8 @@ def tile_list_lens_surface_correction_kernel(
             )
             return raw
 
-        def load_scale_rows_repeated(plane, scales):
-            for q in range(4):
+        def load_scale_rows_repeated(plane, scales, quadrants):
+            for q in quadrants:
                 nc.sync.dma_start(
                     out=plane[32 * q : 32 * (q + 1), :].bitcast(I32),
                     in_=scales[0, 4 * q : 4 * q + 4, :].bitcast(I32).partition_broadcast(8),
@@ -111,9 +112,9 @@ def tile_list_lens_surface_correction_kernel(
         nc.sync.dma_start(out=tab2_w[:], in_=tab2_words[0].rearrange("p t i -> p (t i)").bitcast(I32))
         with nc.allow_non_contiguous_dma(reason="one phase value a partition"):
             nc.scalar.dma_start(out=phase_rows[:], in_=phase[0:512].rearrange("(s p) -> p s", p=P))
-        load_scale_rows_repeated(tab2_s, tab2_scales)
+        load_scale_rows_repeated(tab2_s, tab2_scales, range(4))
         nc.sync.dma_start(out=w4_w[:].bitcast(I32), in_=w4_words[0].bitcast(I32))
-        load_scale_rows_repeated(w4_s, w4_scales)
+        load_scale_rows_repeated(w4_s, w4_scales, range(4))
         nc.sync.dma_start(places[:], pos1)
         nc.sync.dma_start(out=wgs_rows[:], in_=wgs)
         nc.sync.dma_start(idx[:], offs)
@@ -124,26 +125,27 @@ def tile_list_lens_surface_correction_kernel(
         def load_shape_rows(s):
             nc.sync.dma_start(out=s0_rows[s][:], in_=shape0[P * s : P * (s + 1), :])
 
-        w1_raw = [[None, None], [None, None]]
-        for b in range(2):
-            for a in range(2):
-                w1_raw[b][a] = load_weight(w1[512 * a : 512 * (a + 1), 512 * b : 512 * (b + 1)], W1_SLOT[b][a])
-            if b == 1:
-                load_scale_rows(nc.sync, tab_s, tab_scales)
-            load_table(b)
+        def load_w1(b, a):
+            return load_weight(w1[512 * a : 512 * (a + 1), 512 * b : 512 * (b + 1)], W1_SLOT[b][a])
+
+        w1_raw = [[load_w1(0, a) for a in range(2)]]
+        load_table(0)
+        w1_raw.append([load_w1(1, 0)])
+        load_scale_rows(nc.sync, tab_s, tab_scales)
+        load_table(1)
         cosines1 = keep.tile([P, 2 * S + 8], F32, name="cosines1", tag="cos1")
         phase_dealt = cosines1[:, 2 * S : 2 * S + 4]
         with nc.allow_non_contiguous_dma(reason="four phase values a partition"):
             nc.sync.dma_start(out=phase_dealt, in_=phase[512:1024].rearrange("(p t) -> p t", t=4))
-        w2_raw = []
-        for b in range(2):
-            w2_raw.append(load_weight(w2[512 * b : 512 * (b + 1), :], ("late0", "w2_second")[b]))
-            load_shape_rows(b)
+        w1_raw[1].append(load_w1(1, 1))
+        w2_raw = [load_weight(w2[0:512, :], "late0")]
         for q in range(4):
             nc.sync.dma_start(
                 out=wgs_dealt[32 * q : 32 * (q + 1), :, :], in_=wgs.rearrange("(p t) j -> p t j", t=4)
             )
-        for s in range(2, 4):
+        load_shape_rows(0)
+        w2_raw.append(load_weight(w2[512:1024, :], "w2_second"))
+        for s in range(1, 4):
             load_shape_rows(s)
         nc.sync.dma_start(out=s0_dealt[:], in_=shape0[512:1024, :].rearrange("(p t) j -> p t j", t=4))
 
@@ -190,11 +192,11 @@ def tile_list_lens_surface_correction_kernel(
             page = pages[t]
             nc.vector.tensor_tensor(page[:].indirect(places[:]), b_abs[:], weights, MULT)
 
-        def take_cosine(s):
-            nc.scalar.activation(out=cosine(s), in_=pages[s % 4][:, 0:S], func=ACT.Sin, scale=-1.0, bias=half_pi[:])
+        def take_cosine(s, bias=half_pi):
+            nc.scalar.activation(out=cosine(s), in_=pages[s % 4][:, 0:S], func=ACT.Sin, scale=-1.0, bias=bias[:])
 
-        def features(acc, b, t, cols):
-            for a in range(2):
+        def features(acc, b, t, cols, passes=(0, 1)):
+            for a in passes:
                 nc.tensor.matmul_mx(
                     out=acc, lhsT=w1_w[b][a][:, P * t : P * (t + 1)].bitcast(FP8X4),
                     lhsT_scale=w1_s[b][a][:, P * t : P * (t + 1)],
@@ -202,8 +204,8 @@ def tile_list_lens_surface_correction_kernel(
                     start=(a == 0), stop=(a == 1),
                 )
 
-        def first_half_features(s, h):
-            features(banks[(2 * s + h) % 4][:], 0, s, slice(BANK * h, BANK * (h + 1)))
+        def first_half_features(s, h, passes=(0, 1)):
+            features(banks[(2 * s + h) % 4][:], 0, s, slice(BANK * h, BANK * (h + 1)), passes)
 
         def first_half_product(s, h):
             cols = slice(BANK * h, BANK * (h + 1))
@@ -244,12 +246,16 @@ def tile_list_lens_surface_correction_kernel(
             cols = slice(CHUNK * c, CHUNK * (c + 1))
             quantise(z_w[0][:, cols], z_s[0][:, cols], grouped[:])
 
+        def second_half_features(c):
+            start, width = CHUNKS[c]
+            for t in range(4):
+                acc = banks[2 * (c % 2) + t // 2]
+                features(acc[:, width * (t % 2) : width * (t % 2 + 1)], 1, t, slice(start, start + width))
+
         def second_half_products(c, k, prod):
             start, width = CHUNKS[c]
             cols = slice(start, start + width)
             acc = banks[2 * (c % 2) + k]
-            for i in range(2):
-                features(acc[:, width * i : width * (i + 1)], 1, 2 * k + i, cols)
             nc.vector.tensor_tensor(
                 prod[:, 2 * k : 2 * k + 2, 0:width], acc[:, 0 : 2 * width].rearrange("p (t j) -> p t j", t=2),
                 cosines[k][:, 0 : 2 * S].rearrange("p (t j) -> p t j", t=2)[:, :, cols], MULT,
@@ -308,13 +314,16 @@ def tile_list_lens_surface_correction_kernel(
         for s in range(2):
             place_phases(s, b_abs[s])
             take_cosine(s)
-        for a in range(2):
-            quantise(w1_w[0][a][:], w1_s[0][a][:], rounded[a])
+        rounded_first = rounded
         b_abs = [phase_features(s, banks[6 + s % 2]) for s in range(2, 4)]
         rounded = [round_weight(w1_raw[1][a], True) for a in range(2)]
         for s in range(2, 4):
             place_phases(s, b_abs[s - 2])
             take_cosine(s)
+        first_codes = keep.tile([P, 2 * 512], U32, name="first_codes", tag="wgs_rows", align_bytes=64)
+        for a in range(2):
+            w1_w[0].append(first_codes[:, 512 * a : 512 * (a + 1)])
+            quantise(w1_w[0][a], w1_s[0][a][:], rounded_first[a])
         gather(v_w[0][:], tab_w[0][:].bitcast(U32), idx[:])
         quantise(w1_w[1][0][:], w1_s[1][0][:], rounded[0])
         b_abs = [phase_features(s, banks[6 + s % 2]) for s in range(4, 8)]
@@ -323,20 +332,26 @@ def tile_list_lens_surface_correction_kernel(
             gather(v_w[1][:, BANK * h : BANK * (h + 1)], tab_w[1][:].bitcast(U32), idx[:, 32 * h : 32 * (h + 1)])
         waiting = [(w1_w[1], w1_s[1][1], rounded[1])]
         waiting.extend((w2_w, w2_s[b], round_weight(w2_raw[b], False)) for b in range(2))
-        for s in range(2):
+        nc.scalar.activation(
+            out=half_pi_late[:], in_=waiting[2][2][:, 2047:2048], func=ACT.Identity, scale=0.0, bias=half_pi[:]
+        )
+        for a in range(2):
             for h in range(2):
-                first_half_features(s, h)
+                for s in range(2):
+                    first_half_features(s, h, (a,))
         for g in range(2):
-            halves = [(s, h) for s in (2 * g, 2 * g + 1) for h in range(2)]
+            halves = [(s, h) for h in range(2) for s in (2 * g, 2 * g + 1)]
             prods = [first_half_product(s, h) for s, h in halves]
             if g == 0:
                 for s, h in halves:
                     first_half_features(s + 2, h)
+            else:
+                second_half_features(0)
             for (s, h), prod in zip(halves, prods):
                 first_half_turn(s, h, prod)
             for t in (2 * g, 2 * g + 1):
                 place_phases(4 + t, b_abs[t])
-                take_cosine(4 + t)
+                take_cosine(4 + t, half_pi_late)
                 if t < 3:
                     holder, scales, values = waiting[t]
                     codes = keep.tile([P, 512], U32, name="codes", tag="b_abs%d" % t, align_bytes=64)
@@ -348,6 +363,8 @@ def tile_list_lens_surface_correction_kernel(
         grouped = None
         for c in range(len(CHUNKS)):
             prod = keep.tile([P, 4, CHUNK], F32, name="prod4", tag="late%d" % (c % 2))
+            if c + 1 < len(CHUNKS):
+                second_half_features(c + 1)
             second_half_products(c, 0, prod)
             if c > 0:
                 finish_chunk(c - 1, grouped)

import math
from contextlib import ExitStack

import concourse.mybir as mybir
from concourse.masks import make_identity

K, K2, T, T2, S, NP, H, N = 1024, 512, 4096, 2048, 1024, 512, 1024, 512
FLOPS = 2 * (K * H * S + K2 * H * NP + H * N * S)

F32 = mybir.dt.float32
BF16 = mybir.dt.bfloat16
I32 = mybir.dt.int32
U32 = mybir.dt.uint32
U16 = mybir.dt.uint16
U8 = mybir.dt.uint8
FP8X4 = mybir.dt.float8_e4m3fn_x4
FP4X4 = mybir.dt.float4_e2m1fn_x4
ACT = mybir.ActivationFunctionType
MULT = mybir.AluOpType.mult
ADD = mybir.AluOpType.add

P = 128
BANK = 512
CHUNK = 256
W1_SLOT = [["late0", "cos0"], ["cos1", "late1"]]
CHUNKS = [(0, 256), (256, 256), (512, 256), (768, 128), (896, 128)]


def tile_list_lens_surface_correction_kernel(
    tc, tab_words, tab_scales, offs, tab2_words, tab2_scales, offs2, pos1, w1, w4_words, w4_scales,
    phase, wgs, shape0, w2, out,
):
    nc = tc.nc
    with ExitStack() as ctx:
        keep = ctx.enter_context(tc.tile_pool(name="keep", bufs=1))
        ring = ctx.enter_context(tc.tile_pool(name="ring", bufs=2))
        psum = ctx.enter_context(tc.psum_pool(name="psum", bufs=1))

        def kept(name, shape, dtype):
            return keep.tile(shape, dtype, name=name, align_bytes=64)

        banks = [psum.tile([P, BANK], F32, name="bank%d" % i) for i in range(8)]

        idx = keep.tile([P, S // 16], U16, name="idx")
        idx2 = keep.tile([P, NP // 16], U16, name="idx2")
        places = keep.tile([P, NP // 16], U16, name="places")
        tab_w = [kept("tab_w%d" % a, [P, T], I32) for a in range(2)]
        tab_s = kept("tab_s", [P, T], U8)
        tab2_w = kept("tab2_w", [P, T2], I32)
        tab2_s = kept("tab2_s", [P, T2], U8)
        v_w = [kept("v_w%d" % a, [P, S], U32) for a in range(2)]
        v_s = kept("v_s", [P, S], U8)
        v2_w = kept("v2_w", [P, NP], U32)
        v2_s = kept("v2_s", [P, NP], U8)
        w4_w = kept("w4_w", [P, 2 * H], U8)
        w4_s = kept("w4_s", [P, H], U8)
        w4_dealt_w = kept("w4_dealt_w", [P, H], U8)
        w4_dealt_s = kept("w4_dealt_s", [P, H // 2], U8)
        phase_rows = kept("phase_rows", [P, 4], F32)
        wgs_rows = keep.tile([P, NP], F32, name="wgs_rows", tag="wgs_rows", align_bytes=64)
        wgs_dealt = kept("wgs_dealt", [P, 4, NP], F32)
        s0_rows = [keep.tile([P, S], F32, name="s0_rows", tag="rows%d" % s) for s in range(4)]
        s0_dealt = kept("s0_dealt", [P, 4, S], F32)
        w1_w = [[], [kept("w1_w10", [P, 512], U32)]]
        w1_s = [[kept("w1_s%d%d" % (b, a), [P, 512], U8) for a in range(2)] for b in range(2)]
        w2_w = []
        w2_s = [kept("w2_s%d" % b, [P, N], U8) for b in range(2)]
        z_w = [kept("z_w%d" % b, [P, S], U32) for b in range(2)]
        z_s = [kept("z_s%d" % b, [P, S], U8) for b in range(2)]
        pages = [kept("page%d" % i, [P, S + 16], F32) for i in range(4)]
        z_turned = [kept("z_turned%d" % h, [P, 4, 2, P, 2], BF16) for h in range(2)]
        ident = kept("ident", [P, P], F32)
        zero = kept("zero", [P, 1], F32)
        sin_zero = kept("sin_zero", [P, 1], F32)
        half_pi = kept("half_pi", [P, 1], F32)
        half_pi_late = kept("half_pi_late", [P, 1], F32)
        one = kept("one", [P, 1], F32)
        root_one = kept("root_one", [P, 1], F32)

        def load_scale_rows(queue, plane, scales):
            passes = scales.shape[0]
            for q in range(4):
                queue.dma_start(
                    out=plane[32 * q : 32 * q + 4 * passes, :].bitcast(I32),
                    in_=scales[:, 4 * q : 4 * q + 4, :].bitcast(I32),
                )

        def load_weight(rows, tag):
            raw = keep.tile([P, 4 * 512], F32, name="raw", tag=tag)
            nc.sync.dma_start(
                out=raw[:, 0:2048].rearrange("p (j c) -> p j c", j=4), in_=rows.rearrange("(p j) c -> p j c", j=4)
            )
            return raw

        def load_scale_rows_repeated(plane, scales, quadrants):
            for q in quadrants:
                nc.sync.dma_start(
                    out=plane[32 * q : 32 * (q + 1), :].bitcast(I32),
                    in_=scales[0, 4 * q : 4 * q + 4, :].bitcast(I32).partition_broadcast(8),
                )

        nc.vector.memset(zero[:], 0.0)
        nc.vector.memset(one[:], 1.0)
        nc.scalar.activation(out=sin_zero[:], in_=zero[:], func=ACT.Sin)
        nc.gpsimd.memset(tab_s[:].bitcast(I32), 0)
        for i, page in enumerate(pages):
            (nc.vector if i < 2 else nc.gpsimd).memset(page[:], 0.0)
        nc.vector.tensor_scalar_add(half_pi[:], sin_zero[:], math.pi / 2)
        make_identity(nc, ident[:])

        nc.sync.dma_start(idx2[:], offs2)
        nc.sync.dma_start(out=tab2_w[:], in_=tab2_words[0].rearrange("p t i -> p (t i)").bitcast(I32))
        with nc.allow_non_contiguous_dma(reason="one phase value a partition"):
            nc.scalar.dma_start(out=phase_rows[:], in_=phase[0:512].rearrange("(s p) -> p s", p=P))
        load_scale_rows_repeated(tab2_s, tab2_scales, range(4))
        nc.sync.dma_start(out=w4_w[:].bitcast(I32), in_=w4_words[0].bitcast(I32))
        load_scale_rows_repeated(w4_s, w4_scales, range(4))
        nc.sync.dma_start(places[:], pos1)
        nc.sync.dma_start(out=wgs_rows[:], in_=wgs)
        nc.sync.dma_start(idx[:], offs)

        def load_table(a):
            nc.sync.dma_start(out=tab_w[a][:], in_=tab_words[a].rearrange("p t i -> p (t i)").bitcast(I32))

        def load_shape_rows(s):
            nc.sync.dma_start(out=s0_rows[s][:], in_=shape0[P * s : P * (s + 1), :])

        def load_w1(b, a):
            return load_weight(w1[512 * a : 512 * (a + 1), 512 * b : 512 * (b + 1)], W1_SLOT[b][a])

        w1_raw = [[load_w1(0, a) for a in range(2)]]
        load_table(0)
        w1_raw.append([load_w1(1, 0)])
        load_scale_rows(nc.sync, tab_s, tab_scales)
        load_table(1)
        cosines1 = keep.tile([P, 2 * S + 8], F32, name="cosines1", tag="cos1")
        phase_dealt = cosines1[:, 2 * S : 2 * S + 4]
        with nc.allow_non_contiguous_dma(reason="four phase values a partition"):
            nc.sync.dma_start(out=phase_dealt, in_=phase[512:1024].rearrange("(p t) -> p t", t=4))
        w1_raw[1].append(load_w1(1, 1))
        w2_raw = [load_weight(w2[0:512, :], "late0")]
        for q in range(4):
            nc.sync.dma_start(
                out=wgs_dealt[32 * q : 32 * (q + 1), :, :], in_=wgs.rearrange("(p t) j -> p t j", t=4)
            )
        load_shape_rows(0)
        w2_raw.append(load_weight(w2[512:1024, :], "w2_second"))
        for s in range(1, 4):
            load_shape_rows(s)
        nc.sync.dma_start(out=s0_dealt[:], in_=shape0[512:1024, :].rearrange("(p t) j -> p t j", t=4))

        def gather(dst, window, offsets):
            nc.vector.tensor_copy(dst, window.indirect(offsets))

        def quantise(codes, scales, grouped):
            nc.vector.quantize_mx(out=codes.bitcast(FP8X4), scales=scales, in_=grouped)

        def round_weight(raw, deal):
            grouped = ring.tile([P, 512, 4], BF16, name="grouped", bufs=3, align_bytes=64)
            if deal:
                dst = grouped[:].rearrange("p (u e m) j -> p u m j e", u=2, e=2)
                src = raw[:, 0:2048].rearrange("p (j m u e) -> p u m j e", j=4, u=2, e=2)
                for u in range(2):
                    nc.scalar.copy(out=dst[:, u], in_=src[:, u])
                return grouped[:].rearrange("p c j -> p (c j)")
            else:
                dst = grouped[:].rearrange("p (c i) j -> p c j i", i=4)
                src = raw[:, 0:2048].rearrange("p (j c i) -> p c j i", j=4, i=4)
            for half in range(2):
                nc.scalar.copy(out=dst[:, 64 * half : 64 * (half + 1)], in_=src[:, 64 * half : 64 * (half + 1)])
            return grouped[:].rearrange("p c j -> p (c j)")

        def phase_features(s, bank):
            b, t = divmod(s, 4)
            words, scales = (w4_w, w4_s) if b == 0 else (w4_dealt_w, w4_dealt_s)
            bias = (phase_rows, phase_dealt)[b][:, t : t + 1]
            nc.tensor.matmul_mx(
                out=bank[:], lhsT=words[:, 2 * P * t : 2 * P * (t + 1)].bitcast(FP4X4),
                lhsT_scale=scales[:, P * t : P * (t + 1)], rhs=v2_w[:].bitcast(FP8X4), rhs_scale=v2_s[:],
                start=True, stop=True,
            )
            b_abs = keep.tile([P, NP], F32, name="b_abs", tag="b_abs%d" % t, align_bytes=64)
            nc.scalar.activation(out=b_abs[:], in_=bank[:], func=ACT.Abs, bias=bias)
            return b_abs

        def cosine(s):
            return cosines[s % 4 // 2][:, S * (s % 2) : S * (s % 2 + 1)]

        def place_phases(s, b_abs):
            b, t = divmod(s, 4)
            weights = wgs_rows[:] if b == 0 else wgs_dealt[:, t, :]
            page = pages[t]
            nc.vector.tensor_tensor(page[:].indirect(places[:]), b_abs[:], weights, MULT)

        def take_cosine(s, bias=half_pi):
            nc.scalar.activation(out=cosine(s), in_=pages[s % 4][:, 0:S], func=ACT.Sin, scale=-1.0, bias=bias[:])

        def features(acc, b, t, cols, passes=(0, 1)):
            for a in passes:
                nc.tensor.matmul_mx(
                    out=acc, lhsT=w1_w[b][a][:, P * t : P * (t + 1)].bitcast(FP8X4),
                    lhsT_scale=w1_s[b][a][:, P * t : P * (t + 1)],
                    rhs=v_w[a][:, cols].bitcast(FP8X4), rhs_scale=v_s[4 * a : P, cols],
                    start=(a == 0), stop=(a == 1),
                )

        def first_half_features(s, h, passes=(0, 1)):
            features(banks[(2 * s + h) % 4][:], 0, s, slice(BANK * h, BANK * (h + 1)), passes)

        def first_half_product(s, h):
            cols = slice(BANK * h, BANK * (h + 1))
            acc = banks[(2 * s + h) % 4]
            prod = ring.tile([P, BANK], F32, name="prod", bufs=4)
            page = pages[h + 2 * (s // 3)]
            nc.vector.scalar_tensor_tensor(prod[:], acc[:], page[:, S : S + 1], cosine(s)[:, cols], ADD, MULT)
            return prod

        def first_half_turn(s, h, prod):
            turned = banks[4 + (2 * s + h) % 4]
            for jb in range(4):
                blk = slice(P * jb, P * (jb + 1))
                nc.tensor.matmul(
                    turned[:, blk], lhsT=s0_rows[s][:, BANK * h + P * jb : BANK * h + P * (jb + 1)],
                    rhs=ident[:], is_transpose=True, start=True, stop=False,
                )
                nc.tensor.matmul(
                    turned[:, blk], lhsT=prod[:, blk], rhs=ident[:], is_transpose=True, start=False, stop=True
                )
            nc.scalar.copy(
                out=z_turned[h][:, :, :, 32 * s : 32 * (s + 1), :],
                in_=turned[:].rearrange("p (b q u e) -> p b u q e", b=4, u=2, e=2),
            )

        def first_half_back(c):
            h, pair = divmod(c, 2)
            words = z_turned[h][:].rearrange("p b u q e -> p (b u q e)").bitcast(F32)
            bank = banks[6 + c % 2]
            for i in range(4):
                at = P * (4 * pair + i)
                nc.tensor.transpose(bank[:, P * i : P * (i + 1)], words[:, at : at + P], ident[:])
            grouped = ring.tile([P, 4 * CHUNK], BF16, name="z_grouped0", bufs=4, align_bytes=64)
            nc.scalar.copy(
                out=grouped[:].bitcast(F32).rearrange("p (b j u) -> p b j u", b=2, u=2),
                in_=bank[:].rearrange("p (b u j) -> p b j u", b=2, u=2),
            )
            cols = slice(CHUNK * c, CHUNK * (c + 1))
            quantise(z_w[0][:, cols], z_s[0][:, cols], grouped[:])

        def second_half_features(c):
            start, width = CHUNKS[c]
            for t in range(4):
                acc = banks[2 * (c % 2) + t // 2]
                features(acc[:, width * (t % 2) : width * (t % 2 + 1)], 1, t, slice(start, start + width))

        def second_half_products(c, k, prod):
            start, width = CHUNKS[c]
            cols = slice(start, start + width)
            acc = banks[2 * (c % 2) + k]
            nc.vector.tensor_tensor(
                prod[:, 2 * k : 2 * k + 2, 0:width], acc[:, 0 : 2 * width].rearrange("p (t j) -> p t j", t=2),
                cosines[k][:, 0 : 2 * S].rearrange("p (t j) -> p t j", t=2)[:, :, cols], MULT,
            )

        def second_half_sum(c, prod):
            start, width = CHUNKS[c]
            grouped = ring.tile([P, CHUNK, 4], BF16, name="z_grouped1", align_bytes=64)
            nc.vector.tensor_tensor(
                grouped[:, 0:width, :].rearrange("p (c i) t -> p c t i", i=4),
                prod[:, :, 0:width].rearrange("p t (c i) -> p c t i", i=4),
                s0_dealt[:, :, start : start + width].rearrange("p t (c i) -> p c t i", i=4),
                ADD,
            )
            return grouped

        def finish_chunk(c, grouped):
            start, width = CHUNKS[c]
            cols = slice(start, start + width)
            quantise(z_w[1][:, cols], z_s[1][:, cols], grouped[:, 0:width, :].rearrange("p j t -> p (j t)"))
            results = keep.tile([P, 2, BANK], F32, name="results", tag=("rows%d" % c if c < 4 else "w2_second"))
            for k in range(2):
                result = results[:, k, :]
                acc = banks[4 + 2 * (c % 2) + k]
                for i in range(2):
                    n_cols = slice(P * (2 * k + i), P * (2 * k + i + 1))
                    for b in range(2):
                        nc.tensor.matmul_mx(
                            out=acc[:, width * i : width * (i + 1)], lhsT=w2_w[b][:, n_cols].bitcast(FP8X4),
                            lhsT_scale=w2_s[b][:, n_cols], rhs=z_w[b][:, cols].bitcast(FP8X4),
                            rhs_scale=z_s[b][:, cols], start=(b == 0), stop=(b == 1),
                        )
                squares = ring.tile([P, BANK], F32, name="squares")
                nc.scalar.activation(out=squares[:, 0 : 2 * width], in_=acc[:, 0 : 2 * width], func=ACT.Square)
                nc.scalar.activation(
                    out=result[:, 0 : 2 * width], in_=squares[:, 0 : 2 * width], func=ACT.Sqrt, bias=root_one[:]
                )
                nc.sync.dma_start(
                    out=out[2 * P * k : 2 * P * (k + 1), cols].rearrange("(m p) j -> p m j", p=P),
                    in_=result[:, 0 : 2 * width].rearrange("p (m j) -> p m j", m=2),
                )

        gather(v2_w[:], tab2_w[:].bitcast(U32), idx2[:])
        gather(v2_s[:], tab2_s[:], idx2[:])
        nc.vector.tensor_copy(
            w4_dealt_w[:].bitcast(U16).rearrange("p (t m) -> p t m", t=4),
            w4_w[:, H : 2 * H].bitcast(U16).rearrange("p (m t) -> p t m", t=4),
        )
        nc.vector.tensor_copy(
            w4_dealt_s[:].rearrange("p (t m) -> p t m", t=4),
            w4_s[:, H // 2 : H].rearrange("p (m t) -> p t m", t=4),
        )
        b_abs = [phase_features(s, banks[6 + s % 2]) for s in range(2)]
        rounded = [round_weight(w1_raw[0][a], False) for a in range(2)]
        cosines = [keep.tile([P, 2 * S], F32, name="cosines0", tag="cos0"), cosines1]
        for s in range(2):
            place_phases(s, b_abs[s])
            take_cosine(s)
        rounded_first = rounded
        b_abs = [phase_features(s, banks[6 + s % 2]) for s in range(2, 4)]
        rounded = [round_weight(w1_raw[1][a], True) for a in range(2)]
        for s in range(2, 4):
            place_phases(s, b_abs[s - 2])
            take_cosine(s)
        first_codes = keep.tile([P, 2 * 512], U32, name="first_codes", tag="wgs_rows", align_bytes=64)
        for a in range(2):
            w1_w[0].append(first_codes[:, 512 * a : 512 * (a + 1)])
            quantise(w1_w[0][a], w1_s[0][a][:], rounded_first[a])
        gather(v_w[0][:], tab_w[0][:].bitcast(U32), idx[:])
        quantise(w1_w[1][0][:], w1_s[1][0][:], rounded[0])
        b_abs = [phase_features(s, banks[6 + s % 2]) for s in range(4, 8)]
        gather(v_s[:], tab_s[:], idx[:])
        for h in range(2):
            gather(v_w[1][:, BANK * h : BANK * (h + 1)], tab_w[1][:].bitcast(U32), idx[:, 32 * h : 32 * (h + 1)])
        waiting = [(w1_w[1], w1_s[1][1], rounded[1])]
        waiting.extend((w2_w, w2_s[b], round_weight(w2_raw[b], False)) for b in range(2))
        nc.scalar.activation(
            out=half_pi_late[:], in_=waiting[2][2][:, 2047:2048], func=ACT.Identity, scale=0.0, bias=half_pi[:]
        )
        for a in range(2):
            for h in range(2):
                for s in range(2):
                    first_half_features(s, h, (a,))
        for g in range(2):
            halves = [(s, h) for h in range(2) for s in (2 * g, 2 * g + 1)]
            prods = [first_half_product(s, h) for s, h in halves]
            if g == 0:
                for s, h in halves:
                    first_half_features(s + 2, h)
            else:
                second_half_features(0)
            for (s, h), prod in zip(halves, prods):
                first_half_turn(s, h, prod)
            for t in (2 * g, 2 * g + 1):
                place_phases(4 + t, b_abs[t])
                take_cosine(4 + t, half_pi_late)
                if t < 3:
                    holder, scales, values = waiting[t]
                    codes = keep.tile([P, 512], U32, name="codes", tag="b_abs%d" % t, align_bytes=64)
                    holder.append(codes)
                    quantise(codes[:], scales[:], values)
        for c in range(4):
            first_half_back(c)
        nc.scalar.activation(out=root_one[:], in_=cosine(7)[:, 0:1], func=ACT.Sqrt, scale=0.0, bias=one[:])
        grouped = None
        for c in range(len(CHUNKS)):
            prod = keep.tile([P, 4, CHUNK], F32, name="prod4", tag="late%d" % (c % 2))
            if c + 1 < len(CHUNKS):
                second_half_features(c + 1)
            second_half_products(c, 0, prod)
            if c > 0:
                finish_chunk(c - 1, grouped)
            second_half_products(c, 1, prod)
            grouped = second_half_sum(c, prod)
        finish_chunk(len(CHUNKS) - 1, grouped)
